import numpy as np
import ml_dtypes


def mxq(x, axis, fmt="e4m3"):
    dtype, down = {"e4m3": (ml_dtypes.float8_e4m3fn, 7), "e5m2": (ml_dtypes.float8_e5m2, 14)}[fmt]
    v = np.moveaxis(np.asarray(x, np.float32).astype(ml_dtypes.bfloat16).astype(np.float64), axis, -1)
    blocks = v.reshape(v.shape[:-1] + (-1, 32))
    amax = np.abs(blocks).max(-1, keepdims=True)
    byte = np.maximum(np.where(amax > 0, np.frexp(amax)[1] - 1 + 127, 0) - down, 1)
    scale = np.exp2(byte - 127.0)
    codes = (blocks / scale).astype(np.float32).astype(dtype).astype(np.float64)
    return np.moveaxis((codes * scale).reshape(v.shape), -1, axis)


WIDE = False


def mx_kscale(k):
    if not WIDE:
        return np.ones(k)
    levels = np.array([10, -10, 5, -5, 0])
    if k % 512:
        return np.exp2(np.random.permutation(np.resize(levels, k // 32))).repeat(32)
    a = np.empty((k // 512, 16))
    for p in range(k // 512):
        a[p, :8] = np.random.permutation(np.resize(levels, 8))
        for g in range(8):
            far = levels[np.abs(levels - a[p, g]) >= 10]
            a[p, g + 8] = far[np.random.randint(len(far))]
    return np.exp2(a.ravel()).repeat(32)


def f64(x):
    return np.asarray(x).astype(np.float64)


def striped(idx):
    return np.tile(idx.reshape(-1, 16).T, (8, 1)).astype(np.uint16)


def unstriped(offs):
    return offs[:16].T.reshape(-1).astype(np.int64)


E2M1 = np.array([0.0, 0.5, 1.0, 1.5, 2.0, 3.0, 4.0, 6.0, -0.0, -0.5, -1.0, -1.5, -2.0, -3.0, -4.0, -6.0])


def pack_weight(w, fmt):
    k, n = w.shape
    w = f64(np.asarray(w, np.float32).astype(ml_dtypes.bfloat16)).reshape(k // 32, 32, n)
    amax = np.abs(w).max(1)
    if fmt == "e4m3":
        byte = np.frexp(amax)[1] - 1 + 127 - 7
    else:
        mant, ex = np.frexp(amax / 6.0)
        byte = np.where(mant > 0.5, ex, ex - 1) + 127
    byte = np.clip(np.where(amax > 0, byte, 1), 1, 254)
    scaled = (w * np.exp2(127.0 - byte)[:, None, :]).reshape(k, n).astype(np.float32)
    by_word = np.ascontiguousarray(scaled.reshape(k // 512, 128, 4, n).transpose(0, 1, 3, 2))
    if fmt == "e4m3":
        words = by_word.astype(ml_dtypes.float8_e4m3fn).view(np.uint8)
    else:
        c = by_word.astype(ml_dtypes.float4_e2m1fn).view(np.uint8) & 0xF
        words = (c[..., 0::2] | (c[..., 1::2] << 4)).reshape(k // 512, 128, 2 * n)
    return np.ascontiguousarray(words), np.ascontiguousarray(byte.astype(np.uint8).reshape(k // 512, 16, n))


def unpack_weight(words, scales, fmt):
    g, _, n = scales.shape
    words = np.ascontiguousarray(words).reshape(g, 128, n, -1)
    if fmt == "e4m3":
        vals = words.view(ml_dtypes.float8_e4m3fn).astype(np.float64)
    else:
        nib = np.empty((g, 128, n, 4), np.uint8)
        nib[..., 0::2] = words & 0xF
        nib[..., 1::2] = words >> 4
        vals = E2M1[nib]
    vals = vals * np.repeat(np.exp2(scales.astype(np.float64) - 127.0), 8, axis=1)[..., None]
    return vals.transpose(0, 1, 3, 2).reshape(g * 512, n)


def gelu(v):
    return 0.5 * v * (1.0 + np.tanh(np.sqrt(2.0 / np.pi) * (v + 0.044715 * v**3)))


def striped8(idx):
    return np.concatenate([v.reshape(-1, 16).T for v in idx]).astype(np.uint16)


def unstriped8(offs):
    return np.stack([offs[16 * g:16 * g + 16].T.reshape(-1) for g in range(8)]).astype(np.int64)


def runs(v, idx8):
    k = np.arange(v.shape[0])
    return v[k[:, None], idx8[k % 512 // 64]]


def bf(x):
    return np.asarray(x, np.float32).astype(ml_dtypes.bfloat16)


def planes(Y):
    n, m = Y.shape
    b = f64(bf(Y)).reshape(n // 32, 32, m)
    amax = np.abs(b).max(1)
    byte = np.clip(np.where(amax > 0, np.frexp(amax)[1] - 1 + 127 - 7, 1), 1, 254)
    codes = (b * np.exp2(127.0 - byte)[:, None, :]).reshape(n, m).astype(np.float32).astype(ml_dtypes.float8_e4m3fn).view(np.uint8)
    words = codes.reshape(n // 512, 128, 4, m).transpose(0, 1, 3, 2)
    return np.ascontiguousarray(words), np.ascontiguousarray(byte.astype(np.uint8).reshape(n // 512, 16, m))


T, S, P, K, H, N = 2048, 1024, 512, 1024, 1024, 512

def setup_inputs():
    n = np.random.standard_normal
    s = mx_kscale(K)[:, None]
    u = mx_kscale(H)[:, None]
    d = {}
    d["tab_words"], d["tab_scales"] = pack_weight(n((K, T)) * s, "e4m3")
    d["offs"] = striped8(np.stack([np.random.permutation(T)[:S] for _ in range(8)]))
    d["pos1"] = striped(np.random.permutation(S)[:P])
    d["pos2"] = striped(np.random.permutation(S)[:P])
    d["w1"] = (1.5 * n((K, H)) / K ** 0.5 / s * u.T).astype(np.float32)
    d["w2_words"], d["w2_scales"] = pack_weight(n((K, H)) / K ** 0.5 / s, "e2m1")
    d["gain"] = (1.8 * np.exp(0.4 * n(H)) / u[:, 0]).astype(np.float32)
    d["w3"] = (1.2 * n((H, N)) / H ** 0.5 / u * np.exp(0.8 * n(N))).astype(np.float32)
    return d

def reference(tab_words, tab_scales, offs, pos1, pos2, w1, w2_words, w2_scales, gain, w3):
    v = runs(unpack_weight(tab_words, tab_scales, "e4m3"), unstriped8(offs))
    a = mxq(f64(w1), 0, "e4m3").T @ v
    b = unpack_weight(w2_words, w2_scales, "e2m1").T @ v
    h = a / (1.0 + np.square(b))
    first = h[:, unstriped(pos1)]
    second = h[:, unstriped(pos2)]
    z = np.tanh(f64(gain)[:, None] * first) * second
    y = mxq(f64(w3), 0, "e4m3").T @ mxq(z, 0, "e4m3")
    words, scales = planes(y)
    return y, words, scales

@@ -1,0 +1,290 @@
+from contextlib import ExitStack
+
+import concourse.mybir as mybir
+from concourse.masks import make_identity
+
+T, S, M, K, H, N = 2048, 1024, 512, 1024, 1024, 512
+FLOPS = 2 * (2 * K * H * S + H * N * M)
+
+F32 = mybir.dt.float32
+BF16 = mybir.dt.bfloat16
+I32 = mybir.dt.int32
+U32 = mybir.dt.uint32
+U16 = mybir.dt.uint16
+U8 = mybir.dt.uint8
+FP8X4 = mybir.dt.float8_e4m3fn_x4
+FP4X4 = mybir.dt.float4_e2m1fn_x4
+ACT = mybir.ActivationFunctionType
+MULT = mybir.AluOpType.mult
+
+P = 128
+HALF = 512
+CHUNK = 128
+
+
+def tile_list_string_soiling_features_kernel(
+    tc, tab_words, tab_scales, offs, pos1, pos2, w1, w2_words, w2_scales, gain, w3, out_0, out_1, out_2
+):
+    nc = tc.nc
+    with ExitStack() as ctx:
+        lists = ctx.enter_context(tc.tile_pool(name="lists", bufs=1))
+        keep = ctx.enter_context(tc.tile_pool(name="keep", bufs=1))
+        ring = ctx.enter_context(tc.tile_pool(name="ring", bufs=2))
+        psum = ctx.enter_context(tc.psum_pool(name="psum", bufs=4))
+
+        offs_t = lists.tile([P, S // 16], U16, name="offs_t")
+        pos1_t = lists.tile([P, M // 16], U16, name="pos1_t")
+        pos2_t = lists.tile([P, M // 16], U16, name="pos2_t")
+        scale_window = keep.tile([P, T], U8, name="scale_window", align_bytes=64)
+        w2_scale_raw = keep.tile([P, 2, H // 4], I32, name="w2_scale_raw")
+        v_scales = [keep.tile([P, S], U8, name="v_scales%d" % a, align_bytes=64) for a in range(2)]
+        warm_in = keep.tile([P, 1], F32, name="warm_in", tag="late_table")
+        warm_out = keep.tile([P, 1], F32, name="warm_out", tag="stage0")
+
+        nc.gpsimd.memset(scale_window[:].bitcast(I32), 0)
+        nc.vector.memset(warm_in[:], 1.0)
+        nc.vector.memset(w2_scale_raw[:], 0)
+        nc.vector.memset(v_scales[1][:].bitcast(I32), 0)
+        nc.scalar.activation(out=warm_out[:], in_=warm_in[:], func=ACT.Abs_reciprocal_sqrt)
+
+        nc.sync.dma_start(offs_t[:], offs)
+        nc.sync.dma_start(pos1_t[:], pos1)
+        nc.sync.dma_start(pos2_t[:], pos2)
+        for a in range(2):
+            rows = tab_scales[a].bitcast(I32).rearrange("(g e) n -> e g n", e=2)
+            for e in range(2):
+                nc.sync.dma_start(scale_window[:].bitcast(I32)[2 * a + e : P : 16, :], rows[e])
+        table = [
+            keep.tile([P, T], I32, name="table0", tag="stage1"),
+            keep.tile([P, T], I32, name="table1", tag="late_table"),
+        ]
+        w2_raw = keep.tile([P, 2, H // 2], I32, name="w2_raw", tag="stage0")
+        nc.sync.dma_start(table[0][:], tab_words[0].rearrange("p t i -> p (t i)").bitcast(I32))
+        nc.sync.dma_start(w2_raw[:], w2_words.bitcast(I32).rearrange("a p n -> p a n"))
+        nc.sync.dma_start(table[1][:], tab_words[1].rearrange("p t i -> p (t i)").bitcast(I32))
+        for d in range(4):
+            nc.gpsimd.dma_start(
+                w2_scale_raw[32 * d : 32 * d + 4, :, :],
+                w2_scales.bitcast(I32)[:, 4 * d : 4 * d + 4, :].rearrange("a r n -> r a n"),
+            )
+
+        picked_scales = keep.tile([P, S], U8, name="picked_scales", tag="picked", align_bytes=64)
+        nc.vector.tensor_copy(picked_scales[:], scale_window[:].indirect(offs_t[:]))
+        picked32 = picked_scales[:].bitcast(I32)
+        nc.vector.tensor_copy(v_scales[0][:].bitcast(I32), picked32)
+
+        w1_raw = {}
+
+        def load_w1(a, b):
+            raw = keep.tile([P, 4, HALF], F32, name="w1_raw", tag="stage%d" % a)
+            rows = w1[HALF * a : HALF * (a + 1), HALF * b : HALF * (b + 1)]
+            nc.sync.dma_start(raw[:], rows.rearrange("(p j) c -> p j c", j=4))
+            w1_raw[a, b] = raw
+
+        for a in (1, 0):
+            for h in range(2):
+                if a == 0 and h == 0:
+                    continue
+                for e in range(2):
+                    nc.scalar.dma_start(
+                        v_scales[a][:].bitcast(I32)[2 * h + e : P : 32, :],
+                        picked32[16 * h + 2 * a + e : P : 32, :],
+                    )
+
+        w2_codes = keep.tile([P, 4 * 4 * 64], I32, name="w2_codes", align_bytes=64)
+        w2_planes = keep.tile([P, 4 * 4 * 32], I32, name="w2_planes", align_bytes=64)
+        nc.vector.tensor_copy(
+            w2_codes[:].rearrange("p (x t q w) -> p x t q w", x=4, t=4, w=4),
+            w2_raw[:].rearrange("p a n -> p (a n)").rearrange("p (x q t w) -> p x t q w", x=4, t=4, w=4),
+        )
+        load_w1(0, 0)
+
+        v_words = {}
+        for a in range(2):
+            for h in range(2):
+                picked = keep.tile([P, HALF], U32, name="v_words%d%d" % (a, h), align_bytes=64)
+                nc.vector.tensor_copy(
+                    picked[:], table[a][:].bitcast(U32).indirect(offs_t[:, 32 * h : 32 * (h + 1)])
+                )
+                v_words[a, h] = picked
+            if a == 0:
+                nc.vector.tensor_copy(
+                    w2_planes[:].rearrange("p (x t q w) -> p x t q w", x=4, t=4, w=2),
+                    w2_scale_raw[:].rearrange("p a n -> p (a n)").rearrange("p (x q t w) -> p x t q w", x=4, t=4, w=2),
+                )
+
+        load_w1(1, 0)
+
+        def product(u, h, tag, codes, planes):
+            acc = psum.tile([P, HALF], F32, name="acc", tag=tag)
+            for a in range(2):
+                nc.tensor.matmul_mx(
+                    out=acc[:],
+                    lhsT=codes(a),
+                    lhsT_scale=planes(a),
+                    rhs=v_words[a, h][:].bitcast(FP8X4),
+                    rhs_scale=v_scales[a][:, HALF * h : HALF * (h + 1)],
+                    start=(a == 0),
+                    stop=(a == 1),
+                )
+            return acc
+
+        damp = {}
+
+        def damping(u):
+            b, t = divmod(u, 4)
+            w2c = w2_codes[:].bitcast(U8)
+            w2p = w2_planes[:].bitcast(U8)
+            first = lambda a: (8 * a + u) * P
+            tmp = []
+            for h in range(2):
+                acc = product(
+                    u, h, "pb",
+                    lambda a: w2c[:, 2 * first(a) : 2 * (first(a) + P)].bitcast(FP4X4),
+                    lambda a: w2p[:, first(a) : first(a) + P],
+                )
+                sq = ring.tile([P, HALF], F32, name="sq", tag="tmp")
+                nc.scalar.activation(out=sq[:], in_=acc[:], func=ACT.Square)
+                tmp.append(sq)
+            for h in range(2):
+                nc.scalar.activation(out=tmp[h][:], in_=tmp[h][:], func=ACT.Abs_reciprocal_sqrt, bias=1.0)
+            for h in range(2):
+                rec = keep.tile([P, HALF], F32, name="damp%d%d" % (u, h))
+                nc.scalar.activation(out=rec[:], in_=tmp[h][:], func=ACT.Square)
+                damp[u, h] = rec
+
+        w1_q = {}
+
+        def quantize_w1(u, copy):
+            b, t = divmod(u, 4)
+            grouped = ring.tile([P, 2, HALF], BF16, name="w1_grouped", bufs=3, align_bytes=64)
+            for a in range(2):
+                copy(
+                    grouped[:, a, :].rearrange("p (q i j) -> p q i j", i=8, j=4),
+                    w1_raw[a, b][:].rearrange("p j (q t i) -> p t q i j", t=4, i=8)[:, t],
+                )
+            codes = keep.tile([P, 2 * P], U32, name="w1_codes%d" % u, align_bytes=64)
+            planes = keep.tile([P, 2 * P], U8, name="w1_planes%d" % u, align_bytes=64)
+            nc.vector.quantize_mx(
+                out=codes[:].bitcast(FP8X4), scales=planes[:], in_=grouped[:].rearrange("p a c -> p (a c)")
+            )
+            w1_q[u] = (codes, planes)
+
+        firsts = [keep.tile([P, 4, M], F32, name="firsts%d" % b) for b in range(2)]
+        seconds = [keep.tile([P, 4, M], F32, name="seconds%d" % b) for b in range(2)]
+
+        def channels(u):
+            b, t = divmod(u, 4)
+            codes, planes = w1_q[u]
+            h_all = ring.tile([P, S], F32, name="h_all")
+            for h in range(2):
+                acc = product(
+                    u, h, "pa",
+                    lambda a: codes[:, P * a : P * (a + 1)].bitcast(FP8X4),
+                    lambda a: planes[:, P * a : P * (a + 1)],
+                )
+                nc.vector.tensor_tensor(h_all[:, HALF * h : HALF * (h + 1)], acc[:], damp[u, h][:], MULT)
+            nc.vector.tensor_copy(firsts[b][:, t, :], h_all[:].indirect(pos1_t[:]))
+            nc.vector.tensor_copy(seconds[b][:, t, :], h_all[:].indirect(pos2_t[:]))
+
+        w3_q = {}
+
+        def quantize_w3(b):
+            raw = keep.tile([P, 4, N], F32, name="w3_raw", tag="stage%d" % b)
+            rows = w3[HALF * b : HALF * (b + 1), :].rearrange("(q t i) n -> i q t n", t=4, i=8)
+            for i in range(8):
+                nc.sync.dma_start(raw[i:P:8, :, :], rows[i])
+            grouped = ring.tile([P, 4 * N], BF16, name="w3_grouped", align_bytes=64)
+            nc.vector.tensor_copy(
+                grouped[:].rearrange("k (s p j) -> k p s j", s=4, j=4),
+                raw[:].rearrange("k j (p s) -> k p s j", s=4),
+            )
+            codes = keep.tile([P, N], U32, name="w3_codes%d" % b, align_bytes=64)
+            planes = keep.tile([P, N], U8, name="w3_planes%d" % b, align_bytes=64)
+            nc.vector.quantize_mx(out=codes[:].bitcast(FP8X4), scales=planes[:], in_=grouped[:])
+            w3_q[b] = (codes, planes)
+
+        damping(0)
+        damping(1)
+
+        identity = keep.tile([P, P], F32, name="identity")
+        make_identity(nc, identity[:])
+        gain_rows = keep.tile([P, P], F32, name="gain_rows", tag="picked", align_bytes=64)
+        nc.gpsimd.memset(gain_rows[:], 0.0)
+        gain_view = gain.rearrange("(b q t i) -> b t q i", b=2, t=4, i=8)
+        for b in range(2):
+            nc.sync.dma_start(gain_rows[4 * b : 4 * b + 4, :].rearrange("t (q i) -> t q i", i=8), gain_view[b])
+
+        for u in range(4):
+            quantize_w1(u, nc.vector.tensor_copy)
+        load_w1(0, 1)
+        load_w1(1, 1)
+        gains = keep.tile([P, 8], F32, name="gains")
+        for u in range(8):
+            if u + 2 < 8:
+                damping(u + 2)
+            if u < 4:
+                quantize_w1(4 + u, nc.scalar.copy)
+            channels(u)
+            if u == 0:
+                turned = psum.tile([P, P], F32, name="turned", tag="pa")
+                nc.tensor.transpose(turned[:], gain_rows[:], identity[:])
+                nc.vector.tensor_copy(gains[:], turned[:, 0:8])
+            if u in (4, 5):
+                quantize_w3(u - 4)
+
+        z_q = []
+        for b in range(2):
+            bounded = ring.tile([P, 4, M], F32, name="bounded", tag="tmp")
+            for t in range(4):
+                u = 4 * b + t
+                nc.scalar.activation(
+                    out=bounded[:, t, :], in_=firsts[b][:, t, :], func=ACT.Tanh, scale=gains[:, u : u + 1]
+                )
+            codes = keep.tile([P, M], U32, name="z_codes%d" % b, align_bytes=64)
+            planes = keep.tile([P, M], U8, name="z_planes%d" % b, align_bytes=64)
+            for c in range(M // CHUNK):
+                cols = slice(CHUNK * c, CHUNK * (c + 1))
+                z = ring.tile([P, 4 * CHUNK], BF16, name="z", bufs=4, align_bytes=64)
+                nc.vector.tensor_tensor(
+                    z[:].rearrange("p (c i t) -> p c t i", i=4, t=4),
+                    bounded[:, :, cols].rearrange("p t (c i) -> p c t i", i=4),
+                    seconds[b][:, :, cols].rearrange("p t (c i) -> p c t i", i=4),
+                    MULT,
+                )
+                nc.vector.quantize_mx(out=codes[:, cols].bitcast(FP8X4), scales=planes[:, cols], in_=z[:])
+            z_q.append((codes, planes))
+
+        y_codes = keep.tile([P, M], U32, name="y_codes", align_bytes=64)
+        y_planes = keep.tile([P, M], U8, name="y_planes", align_bytes=64)
+        out_rows = out_0.rearrange("(p s) m -> p s m", s=4)
+        out_words = out_1[0].rearrange("p m t -> p (m t)").bitcast(I32)
+        for c in range(M // CHUNK):
+            cols = slice(CHUNK * c, CHUNK * (c + 1))
+            acc = psum.tile([P, 4, CHUNK], F32, name="y_acc", tag="pb")
+            for s in range(4):
+                for b in range(2):
+                    nc.tensor.matmul_mx(
+                        out=acc[:, s, :],
+                        lhsT=w3_q[b][0][:, P * s : P * (s + 1)].bitcast(FP8X4),
+                        lhsT_scale=w3_q[b][1][:, P * s : P * (s + 1)],
+                        rhs=z_q[b][0][:, cols].bitcast(FP8X4),
+                        rhs_scale=z_q[b][1][:, cols],
+                        start=(b == 0),
+                        stop=(b == 1),
+                    )
+            y = ring.tile([P, 4, CHUNK], F32, name="y", bufs=4)
+            nc.scalar.copy(y[:], acc[:])
+            nc.sync.dma_start(out_rows[:, :, cols], y[:])
+            y_grouped = ring.tile([P, 4 * CHUNK], BF16, name="y_grouped", bufs=4, align_bytes=64)
+            nc.vector.tensor_copy(
+                y_grouped[:].rearrange("p (c i s) -> p c s i", i=4, s=4),
+                y[:].rearrange("p s (c i) -> p c s i", i=4),
+            )
+            nc.vector.quantize_mx(out=y_codes[:, cols].bitcast(FP8X4), scales=y_planes[:, cols], in_=y_grouped[:])
+            nc.sync.dma_start(out_words[:, cols], y_codes[:, cols].bitcast(I32))
+        for d in range(4):
+            queue = nc.sync if d % 2 == 0 else nc.scalar
+            queue.dma_start(
+                out_2[0].bitcast(I32)[4 * d : 4 * d + 4, :], y_planes[:].bitcast(I32)[32 * d : 32 * d + 4, :]
+            )

@@ -30,12 +30,13 @@ def tile_list_string_soiling_features_kernel(
         lists = ctx.enter_context(tc.tile_pool(name="lists", bufs=1))
         keep = ctx.enter_context(tc.tile_pool(name="keep", bufs=1))
         ring = ctx.enter_context(tc.tile_pool(name="ring", bufs=2))
+        stage = ctx.enter_context(tc.tile_pool(name="stage", bufs=1))
         psum = ctx.enter_context(tc.psum_pool(name="psum", bufs=4))
 
         offs_t = lists.tile([P, S // 16], U16, name="offs_t")
         pos1_t = lists.tile([P, M // 16], U16, name="pos1_t")
         pos2_t = lists.tile([P, M // 16], U16, name="pos2_t")
-        scale_window = keep.tile([P, T], U8, name="scale_window", align_bytes=64)
+        scale_window = keep.tile([P, T], U8, name="scale_window", tag="window", align_bytes=64)
         w2_scale_raw = keep.tile([P, 2, H // 4], I32, name="w2_scale_raw")
         v_scales = [keep.tile([P, S], U8, name="v_scales%d" % a, align_bytes=64) for a in range(2)]
         warm_in = keep.tile([P, 1], F32, name="warm_in", tag="late_table")
@@ -45,7 +46,6 @@ def tile_list_string_soiling_features_kernel(
         nc.vector.memset(warm_in[:], 1.0)
         nc.vector.memset(w2_scale_raw[:], 0)
         nc.vector.memset(v_scales[1][:].bitcast(I32), 0)
-        nc.scalar.activation(out=warm_out[:], in_=warm_in[:], func=ACT.Abs_reciprocal_sqrt)
 
         nc.sync.dma_start(offs_t[:], offs)
         nc.sync.dma_start(pos1_t[:], pos1)
@@ -53,9 +53,24 @@ def tile_list_string_soiling_features_kernel(
         for a in range(2):
             rows = tab_scales[a].bitcast(I32).rearrange("(g e) n -> e g n", e=2)
             for e in range(2):
-                nc.sync.dma_start(scale_window[:].bitcast(I32)[2 * a + e : P : 16, :], rows[e])
+                nc.scalar.dma_start(scale_window[:].bitcast(I32)[2 * a + e : P : 16, :], rows[e])
+        nc.scalar.activation(out=warm_out[:], in_=warm_in[:], func=ACT.Abs_reciprocal_sqrt)
+
+        w1_raw = {}
+
+        def staging(x):
+            if x == 0:
+                return keep.tile([P, 4, HALF], F32, name="raw0", tag="stage0")
+            return stage.tile([P, 4, HALF], F32, name="raw1", offset=2048)
+
+        def load_w1(a, b):
+            raw = staging(a)
+            rows = w1[HALF * a : HALF * (a + 1), HALF * b : HALF * (b + 1)]
+            nc.sync.dma_start(raw[:], rows.rearrange("(p j) c -> p j c", j=4))
+            w1_raw[a, b] = raw
+
         table = [
-            keep.tile([P, T], I32, name="table0", tag="stage1"),
+            stage.tile([P, T], I32, name="table0", offset=1024),
             keep.tile([P, T], I32, name="table1", tag="late_table"),
         ]
         w2_raw = keep.tile([P, 2, H // 2], I32, name="w2_raw", tag="stage0")
@@ -73,14 +88,6 @@ def tile_list_string_soiling_features_kernel(
         picked32 = picked_scales[:].bitcast(I32)
         nc.vector.tensor_copy(v_scales[0][:].bitcast(I32), picked32)
 
-        w1_raw = {}
-
-        def load_w1(a, b):
-            raw = keep.tile([P, 4, HALF], F32, name="w1_raw", tag="stage%d" % a)
-            rows = w1[HALF * a : HALF * (a + 1), HALF * b : HALF * (b + 1)]
-            nc.sync.dma_start(raw[:], rows.rearrange("(p j) c -> p j c", j=4))
-            w1_raw[a, b] = raw
-
         for a in (1, 0):
             for h in range(2):
                 if a == 0 and h == 0:
@@ -92,28 +99,25 @@ def tile_list_string_soiling_features_kernel(
                     )
 
         w2_codes = keep.tile([P, 4 * 4 * 64], I32, name="w2_codes", align_bytes=64)
-        w2_planes = keep.tile([P, 4 * 4 * 32], I32, name="w2_planes", align_bytes=64)
+        w2_planes = stage.tile([P, 4 * 4 * 32], I32, name="w2_planes", offset=0, align_bytes=64)
         nc.vector.tensor_copy(
             w2_codes[:].rearrange("p (x t q w) -> p x t q w", x=4, t=4, w=4),
             w2_raw[:].rearrange("p a n -> p (a n)").rearrange("p (x q t w) -> p x t q w", x=4, t=4, w=4),
         )
         load_w1(0, 0)
 
-        v_words = {}
-        for a in range(2):
-            for h in range(2):
-                picked = keep.tile([P, HALF], U32, name="v_words%d%d" % (a, h), align_bytes=64)
-                nc.vector.tensor_copy(
-                    picked[:], table[a][:].bitcast(U32).indirect(offs_t[:, 32 * h : 32 * (h + 1)])
-                )
-                v_words[a, h] = picked
-            if a == 0:
-                nc.vector.tensor_copy(
-                    w2_planes[:].rearrange("p (x t q w) -> p x t q w", x=4, t=4, w=2),
-                    w2_scale_raw[:].rearrange("p a n -> p (a n)").rearrange("p (x q t w) -> p x t q w", x=4, t=4, w=2),
-                )
-
+        first_words = keep.tile([P, S], U32, name="first_words", tag="window", align_bytes=64)
+        nc.vector.tensor_copy(first_words[:], table[0][:].bitcast(U32).indirect(offs_t[:]))
+        v_words = {(0, h): first_words[:, HALF * h : HALF * (h + 1)] for h in range(2)}
         load_w1(1, 0)
+        nc.vector.tensor_copy(
+            w2_planes[:].rearrange("p (x t q w) -> p x t q w", x=4, t=4, w=2),
+            w2_scale_raw[:].rearrange("p a n -> p (a n)").rearrange("p (x q t w) -> p x t q w", x=4, t=4, w=2),
+        )
+        for h in range(2):
+            picked = keep.tile([P, HALF], U32, name="second_words%d" % h, align_bytes=64)
+            nc.vector.tensor_copy(picked[:], table[1][:].bitcast(U32).indirect(offs_t[:, 32 * h : 32 * (h + 1)]))
+            v_words[1, h] = picked[:]
 
         def product(u, h, tag, codes, planes):
             acc = psum.tile([P, HALF], F32, name="acc", tag=tag)
@@ -122,7 +126,7 @@ def tile_list_string_soiling_features_kernel(
                     out=acc[:],
                     lhsT=codes(a),
                     lhsT_scale=planes(a),
-                    rhs=v_words[a, h][:].bitcast(FP8X4),
+                    rhs=v_words[a, h].bitcast(FP8X4),
                     rhs_scale=v_scales[a][:, HALF * h : HALF * (h + 1)],
                     start=(a == 0),
                     stop=(a == 1),
@@ -155,14 +159,19 @@ def tile_list_string_soiling_features_kernel(
 
         w1_q = {}
 
-        def quantize_w1(u, copy):
+        w1_grouped = {}
+
+        def round_w1(u, a, copy):
             b, t = divmod(u, 4)
-            grouped = ring.tile([P, 2, HALF], BF16, name="w1_grouped", bufs=3, align_bytes=64)
-            for a in range(2):
-                copy(
-                    grouped[:, a, :].rearrange("p (q i j) -> p q i j", i=8, j=4),
-                    w1_raw[a, b][:].rearrange("p j (q t i) -> p t q i j", t=4, i=8)[:, t],
-                )
+            if a == 0:
+                w1_grouped[u] = ring.tile([P, 2, HALF], BF16, name="w1_grouped", bufs=4, align_bytes=64)
+            copy(
+                w1_grouped[u][:, a, :].rearrange("p (q x i j) -> p q x j i", x=2, i=4, j=4),
+                w1_raw[a, b][:].rearrange("p j (q t x i) -> p t q x j i", t=4, x=2, i=4)[:, t],
+            )
+
+        def quantize_w1(u):
+            grouped = w1_grouped[u]
             codes = keep.tile([P, 2 * P], U32, name="w1_codes%d" % u, align_bytes=64)
             planes = keep.tile([P, 2 * P], U8, name="w1_planes%d" % u, align_bytes=64)
             nc.vector.quantize_mx(
@@ -190,20 +199,22 @@ def tile_list_string_soiling_features_kernel(
         w3_q = {}
 
         def quantize_w3(b):
-            raw = keep.tile([P, 4, N], F32, name="w3_raw", tag="stage%d" % b)
+            raw = staging(b)
             rows = w3[HALF * b : HALF * (b + 1), :].rearrange("(q t i) n -> i q t n", t=4, i=8)
             for i in range(8):
                 nc.sync.dma_start(raw[i:P:8, :, :], rows[i])
             grouped = ring.tile([P, 4 * N], BF16, name="w3_grouped", align_bytes=64)
-            nc.vector.tensor_copy(
-                grouped[:].rearrange("k (s p j) -> k p s j", s=4, j=4),
-                raw[:].rearrange("k j (p s) -> k p s j", s=4),
+            nc.scalar.copy(
+                grouped[:].rearrange("k (s p j) -> k p j s", s=4, j=4),
+                raw[:].rearrange("k j (p s) -> k p j s", s=4),
             )
             codes = keep.tile([P, N], U32, name="w3_codes%d" % b, align_bytes=64)
             planes = keep.tile([P, N], U8, name="w3_planes%d" % b, align_bytes=64)
             nc.vector.quantize_mx(out=codes[:].bitcast(FP8X4), scales=planes[:], in_=grouped[:])
             w3_q[b] = (codes, planes)
 
+        for u in range(4):
+            round_w1(u, 0, nc.vector.tensor_copy)
         damping(0)
         damping(1)
 
@@ -216,7 +227,8 @@ def tile_list_string_soiling_features_kernel(
             nc.sync.dma_start(gain_rows[4 * b : 4 * b + 4, :].rearrange("t (q i) -> t q i", i=8), gain_view[b])
 
         for u in range(4):
-            quantize_w1(u, nc.vector.tensor_copy)
+            round_w1(u, 1, nc.vector.tensor_copy)
+            quantize_w1(u)
         load_w1(0, 1)
         load_w1(1, 1)
         gains = keep.tile([P, 8], F32, name="gains")
@@ -224,14 +236,16 @@ def tile_list_string_soiling_features_kernel(
             if u + 2 < 8:
                 damping(u + 2)
             if u < 4:
-                quantize_w1(4 + u, nc.scalar.copy)
+                round_w1(4 + u, 0, nc.scalar.copy)
+                round_w1(4 + u, 1, nc.scalar.copy)
+                quantize_w1(4 + u)
             channels(u)
             if u == 0:
                 turned = psum.tile([P, P], F32, name="turned", tag="pa")
                 nc.tensor.transpose(turned[:], gain_rows[:], identity[:])
                 nc.vector.tensor_copy(gains[:], turned[:, 0:8])
-            if u in (4, 5):
-                quantize_w3(u - 4)
+            if u in (5, 6):
+                quantize_w3(u - 5)
 
         z_q = []
         for b in range(2):
@@ -243,9 +257,10 @@ def tile_list_string_soiling_features_kernel(
                 )
             codes = keep.tile([P, M], U32, name="z_codes%d" % b, align_bytes=64)
             planes = keep.tile([P, M], U8, name="z_planes%d" % b, align_bytes=64)
-            for c in range(M // CHUNK):
-                cols = slice(CHUNK * c, CHUNK * (c + 1))
-                z = ring.tile([P, 4 * CHUNK], BF16, name="z", bufs=4, align_bytes=64)
+            width = M if b == 0 else CHUNK
+            for c in range(M // width):
+                cols = slice(width * c, width * (c + 1))
+                z = ring.tile([P, 4 * width], BF16, name="z", tag="z%d" % b, bufs=1 + 3 * b, align_bytes=64)
                 nc.vector.tensor_tensor(
                     z[:].rearrange("p (c i t) -> p c t i", i=4, t=4),
                     bounded[:, :, cols].rearrange("p t (c i) -> p c t i", i=4),

@@ -16,6 +16,7 @@ FP8X4 = mybir.dt.float8_e4m3fn_x4
 FP4X4 = mybir.dt.float4_e2m1fn_x4
 ACT = mybir.ActivationFunctionType
 MULT = mybir.AluOpType.mult
+ADD = mybir.AluOpType.add
 
 P = 128
 HALF = 512
@@ -40,10 +41,12 @@ def tile_list_string_soiling_features_kernel(
         w2_scale_raw = keep.tile([P, 2, H // 4], I32, name="w2_scale_raw")
         v_scales = [keep.tile([P, S], U8, name="v_scales%d" % a, align_bytes=64) for a in range(2)]
         warm_in = keep.tile([P, 1], F32, name="warm_in", tag="late_table")
-        warm_out = keep.tile([P, 1], F32, name="warm_out", tag="stage0")
+        warm_bias = stage.tile([P, 1], F32, name="warm_bias", offset=0)
+        warm_out = stage.tile([P, 1], F32, name="warm_out", offset=8192)
 
         nc.gpsimd.memset(scale_window[:].bitcast(I32), 0)
         nc.vector.memset(warm_in[:], 1.0)
+        nc.vector.memset(warm_bias[:], 1.0)
         nc.vector.memset(w2_scale_raw[:], 0)
         nc.vector.memset(v_scales[1][:].bitcast(I32), 0)
 
@@ -54,14 +57,12 @@ def tile_list_string_soiling_features_kernel(
             rows = tab_scales[a].bitcast(I32).rearrange("(g e) n -> e g n", e=2)
             for e in range(2):
                 nc.scalar.dma_start(scale_window[:].bitcast(I32)[2 * a + e : P : 16, :], rows[e])
-        nc.scalar.activation(out=warm_out[:], in_=warm_in[:], func=ACT.Abs_reciprocal_sqrt)
+        nc.scalar.activation(out=warm_out[:], in_=warm_in[:], func=ACT.Abs_reciprocal_sqrt, bias=warm_bias[:])
 
         w1_raw = {}
 
         def staging(x):
-            if x == 0:
-                return keep.tile([P, 4, HALF], F32, name="raw0", tag="stage0")
-            return stage.tile([P, 4, HALF], F32, name="raw1", offset=2048)
+            return stage.tile([P, 4, HALF], F32, name="raw", tag="raw%d" % x, offset=8192 * x)
 
         def load_w1(a, b):
             raw = staging(a)
@@ -70,13 +71,14 @@ def tile_list_string_soiling_features_kernel(
             w1_raw[a, b] = raw
 
         table = [
-            stage.tile([P, T], I32, name="table0", offset=1024),
+            keep.tile([P, T], I32, name="table0", tag="early_table", align_bytes=64),
             keep.tile([P, T], I32, name="table1", tag="late_table"),
         ]
-        w2_raw = keep.tile([P, 2, H // 2], I32, name="w2_raw", tag="stage0")
+        w2_raw = stage.tile([P, 2, H // 2], I32, name="w2_raw", offset=8192)
         nc.sync.dma_start(table[0][:], tab_words[0].rearrange("p t i -> p (t i)").bitcast(I32))
         nc.sync.dma_start(w2_raw[:], w2_words.bitcast(I32).rearrange("a p n -> p a n"))
         nc.sync.dma_start(table[1][:], tab_words[1].rearrange("p t i -> p (t i)").bitcast(I32))
+        load_w1(0, 0)
         for d in range(4):
             nc.gpsimd.dma_start(
                 w2_scale_raw[32 * d : 32 * d + 4, :, :],
@@ -99,17 +101,16 @@ def tile_list_string_soiling_features_kernel(
                     )
 
         w2_codes = keep.tile([P, 4 * 4 * 64], I32, name="w2_codes", align_bytes=64)
-        w2_planes = stage.tile([P, 4 * 4 * 32], I32, name="w2_planes", offset=0, align_bytes=64)
+        w2_planes = keep.tile([P, 4 * 4 * 32], I32, name="w2_planes", tag="early_table", align_bytes=64)
         nc.vector.tensor_copy(
             w2_codes[:].rearrange("p (x t q w) -> p x t q w", x=4, t=4, w=4),
             w2_raw[:].rearrange("p a n -> p (a n)").rearrange("p (x q t w) -> p x t q w", x=4, t=4, w=4),
         )
-        load_w1(0, 0)
+        load_w1(1, 0)
 
         first_words = keep.tile([P, S], U32, name="first_words", tag="window", align_bytes=64)
         nc.vector.tensor_copy(first_words[:], table[0][:].bitcast(U32).indirect(offs_t[:]))
         v_words = {(0, h): first_words[:, HALF * h : HALF * (h + 1)] for h in range(2)}
-        load_w1(1, 0)
         nc.vector.tensor_copy(
             w2_planes[:].rearrange("p (x t q w) -> p x t q w", x=4, t=4, w=2),
             w2_scale_raw[:].rearrange("p a n -> p (a n)").rearrange("p (x q t w) -> p x t q w", x=4, t=4, w=2),
@@ -134,28 +135,38 @@ def tile_list_string_soiling_features_kernel(
             return acc
 
         damp = {}
+        picks = [keep.tile([P, 4, 2, M], F32, name="picks%d" % b) for b in range(2)]
 
         def damping(u):
             b, t = divmod(u, 4)
             w2c = w2_codes[:].bitcast(U8)
             w2p = w2_planes[:].bitcast(U8)
             first = lambda a: (8 * a + u) * P
-            tmp = []
+            if u < 7:
+                sq = ring.tile([P, S], F32, name="sq")
+            else:
+                sq = keep.tile([P, S], F32, name="sq_last", tag="last")
             for h in range(2):
                 acc = product(
                     u, h, "pb",
                     lambda a: w2c[:, 2 * first(a) : 2 * (first(a) + P)].bitcast(FP4X4),
                     lambda a: w2p[:, first(a) : first(a) + P],
                 )
-                sq = ring.tile([P, HALF], F32, name="sq", tag="tmp")
-                nc.scalar.activation(out=sq[:], in_=acc[:], func=ACT.Square)
-                tmp.append(sq)
-            for h in range(2):
-                nc.scalar.activation(out=tmp[h][:], in_=tmp[h][:], func=ACT.Abs_reciprocal_sqrt, bias=1.0)
-            for h in range(2):
-                rec = keep.tile([P, HALF], F32, name="damp%d%d" % (u, h))
-                nc.scalar.activation(out=rec[:], in_=tmp[h][:], func=ACT.Square)
-                damp[u, h] = rec
+                nc.scalar.activation(out=sq[:, HALF * h : HALF * (h + 1)], in_=acc[:], func=ACT.Square)
+            width = HALF if u == 0 else S
+            for c in range(0, S, width):
+                cols = slice(c, c + width)
+                nc.scalar.activation(out=sq[:, cols], in_=sq[:, cols], func=ACT.Abs_reciprocal_sqrt, bias=1.0)
+            if u < 2:
+                rec = keep.tile([P, 2, HALF], F32, name="damp%d" % u)[:]
+            else:
+                rec = picks[(u - 1) // 4][:, (u - 1) % 4, :, :]
+            if u == 0:
+                for h in range(2):
+                    nc.scalar.activation(out=rec[:, h, :], in_=sq[:, HALF * h : HALF * (h + 1)], func=ACT.Square)
+            else:
+                nc.scalar.activation(out=rec, in_=sq[:].rearrange("p (h c) -> p h c", h=2), func=ACT.Square)
+            damp[u] = rec
 
         w1_q = {}
 
@@ -165,6 +176,13 @@ def tile_list_string_soiling_features_kernel(
             b, t = divmod(u, 4)
             if a == 0:
                 w1_grouped[u] = ring.tile([P, 2, HALF], BF16, name="w1_grouped", bufs=4, align_bytes=64)
+            if copy is None:
+                nc.gpsimd.tensor_scalar(
+                    w1_grouped[u][:, a, :].rearrange("p (q i j) -> p q i j", i=8, j=4),
+                    w1_raw[a, b][:].rearrange("p j (q t i) -> p t q i j", t=4, i=8)[:, t],
+                    1.0, 0.0, MULT, ADD,
+                )
+                return
             copy(
                 w1_grouped[u][:, a, :].rearrange("p (q x i j) -> p q x j i", x=2, i=4, j=4),
                 w1_raw[a, b][:].rearrange("p j (q t x i) -> p t q x j i", t=4, x=2, i=4)[:, t],
@@ -179,22 +197,26 @@ def tile_list_string_soiling_features_kernel(
             )
             w1_q[u] = (codes, planes)
 
-        firsts = [keep.tile([P, 4, M], F32, name="firsts%d" % b) for b in range(2)]
-        seconds = [keep.tile([P, 4, M], F32, name="seconds%d" % b) for b in range(2)]
+
+        h_tiles = {}
 
         def channels(u):
             b, t = divmod(u, 4)
             codes, planes = w1_q[u]
-            h_all = ring.tile([P, S], F32, name="h_all")
+            h_all = ring.tile([P, S], F32, name="h_all", bufs=3)
             for h in range(2):
                 acc = product(
                     u, h, "pa",
                     lambda a: codes[:, P * a : P * (a + 1)].bitcast(FP8X4),
                     lambda a: planes[:, P * a : P * (a + 1)],
                 )
-                nc.vector.tensor_tensor(h_all[:, HALF * h : HALF * (h + 1)], acc[:], damp[u, h][:], MULT)
-            nc.vector.tensor_copy(firsts[b][:, t, :], h_all[:].indirect(pos1_t[:]))
-            nc.vector.tensor_copy(seconds[b][:, t, :], h_all[:].indirect(pos2_t[:]))
+                nc.vector.tensor_tensor(h_all[:, HALF * h : HALF * (h + 1)], acc[:], damp[u][:, h, :], MULT)
+            h_tiles[u] = h_all
+
+        def pick(u):
+            b, t = divmod(u, 4)
+            nc.vector.tensor_copy(picks[b][:, t, 0, :], h_tiles[u][:].indirect(pos1_t[:]))
+            nc.vector.tensor_copy(picks[b][:, t, 1, :], h_tiles[u][:].indirect(pos2_t[:]))
 
         w3_q = {}
 
@@ -214,7 +236,7 @@ def tile_list_string_soiling_features_kernel(
             w3_q[b] = (codes, planes)
 
         for u in range(4):
-            round_w1(u, 0, nc.vector.tensor_copy)
+            round_w1(u, 0, nc.scalar.copy)
         damping(0)
         damping(1)
 
@@ -231,30 +253,37 @@ def tile_list_string_soiling_features_kernel(
             quantize_w1(u)
         load_w1(0, 1)
         load_w1(1, 1)
-        gains = keep.tile([P, 8], F32, name="gains")
         for u in range(8):
             if u + 2 < 8:
                 damping(u + 2)
-            if u < 4:
-                round_w1(4 + u, 0, nc.scalar.copy)
-                round_w1(4 + u, 1, nc.scalar.copy)
-                quantize_w1(4 + u)
             channels(u)
             if u == 0:
-                turned = psum.tile([P, P], F32, name="turned", tag="pa")
+                pick(0)
+            if u >= 2:
+                pick(u - 1)
+            if u < 4:
+                round_w1(4 + u, 0, None)
+                round_w1(4 + u, 1, None)
+                quantize_w1(4 + u)
+            if u == 5:
+                turned = psum.tile([P, P], F32, name="turned", tag="pb")
                 nc.tensor.transpose(turned[:], gain_rows[:], identity[:])
-                nc.vector.tensor_copy(gains[:], turned[:, 0:8])
-            if u in (5, 6):
-                quantize_w3(u - 5)
+                gains = keep.tile([P, 8], F32, name="gains", tag="last")
+                nc.scalar.copy(gains[:], turned[:, 0:8])
+
+        pick(7)
 
         z_q = []
         for b in range(2):
-            bounded = ring.tile([P, 4, M], F32, name="bounded", tag="tmp")
+            bounded = ring.tile([P, 4, M], F32, name="bounded")
             for t in range(4):
                 u = 4 * b + t
                 nc.scalar.activation(
-                    out=bounded[:, t, :], in_=firsts[b][:, t, :], func=ACT.Tanh, scale=gains[:, u : u + 1]
+                    out=bounded[:, t, :], in_=picks[b][:, t, 0, :], func=ACT.Tanh, scale=gains[:, u : u + 1]
                 )
+            if b == 0:
+                quantize_w3(0)
+                quantize_w3(1)
             codes = keep.tile([P, M], U32, name="z_codes%d" % b, align_bytes=64)
             planes = keep.tile([P, M], U8, name="z_planes%d" % b, align_bytes=64)
             width = M if b == 0 else CHUNK
@@ -264,7 +293,7 @@ def tile_list_string_soiling_features_kernel(
                 nc.vector.tensor_tensor(
                     z[:].rearrange("p (c i t) -> p c t i", i=4, t=4),
                     bounded[:, :, cols].rearrange("p t (c i) -> p c t i", i=4),
-                    seconds[b][:, :, cols].rearrange("p t (c i) -> p c t i", i=4),
+                    picks[b][:, :, 1, cols].rearrange("p t (c i) -> p c t i", i=4),
                     MULT,
                 )
                 nc.vector.quantize_mx(out=codes[:, cols].bitcast(FP8X4), scales=planes[:, cols], in_=z[:])

@@ -38,11 +38,11 @@ def tile_list_string_soiling_features_kernel(
         pos1_t = lists.tile([P, M // 16], U16, name="pos1_t")
         pos2_t = lists.tile([P, M // 16], U16, name="pos2_t")
         scale_window = keep.tile([P, T], U8, name="scale_window", tag="window", align_bytes=64)
-        w2_scale_raw = keep.tile([P, 2, H // 4], I32, name="w2_scale_raw")
+        w2_scale_raw = keep.tile([P, 2, H // 4], I32, name="w2_scale_raw", tag="late", align_bytes=64)
         v_scales = [keep.tile([P, S], U8, name="v_scales%d" % a, align_bytes=64) for a in range(2)]
         warm_in = keep.tile([P, 1], F32, name="warm_in", tag="late_table")
         warm_bias = stage.tile([P, 1], F32, name="warm_bias", offset=0)
-        warm_out = stage.tile([P, 1], F32, name="warm_out", offset=8192)
+        warm_out = stage.tile([P, 1], F32, name="warm_out", offset=14336)
 
         nc.gpsimd.memset(scale_window[:].bitcast(I32), 0)
         nc.vector.memset(warm_in[:], 1.0)
@@ -65,16 +65,19 @@ def tile_list_string_soiling_features_kernel(
             return stage.tile([P, 4, HALF], F32, name="raw", tag="raw%d" % x, offset=8192 * x)
 
         def load_w1(a, b):
-            raw = staging(a)
+            if b == 0:
+                raw = staging(a)
+            else:
+                raw = keep.tile([P, 4, HALF], F32, name="w1_late", tag=("early_table", "late_table")[a])
             rows = w1[HALF * a : HALF * (a + 1), HALF * b : HALF * (b + 1)]
             nc.sync.dma_start(raw[:], rows.rearrange("(p j) c -> p j c", j=4))
             w1_raw[a, b] = raw
 
         table = [
-            keep.tile([P, T], I32, name="table0", tag="early_table", align_bytes=64),
+            keep.tile([P, T], I32, name="table0", tag="early_table"),
             keep.tile([P, T], I32, name="table1", tag="late_table"),
         ]
-        w2_raw = stage.tile([P, 2, H // 2], I32, name="w2_raw", offset=8192)
+        w2_raw = stage.tile([P, 2, H // 2], I32, name="w2_raw", offset=14336)
         nc.sync.dma_start(table[0][:], tab_words[0].rearrange("p t i -> p (t i)").bitcast(I32))
         nc.sync.dma_start(w2_raw[:], w2_words.bitcast(I32).rearrange("a p n -> p a n"))
         nc.sync.dma_start(table[1][:], tab_words[1].rearrange("p t i -> p (t i)").bitcast(I32))
@@ -101,24 +104,27 @@ def tile_list_string_soiling_features_kernel(
                     )
 
         w2_codes = keep.tile([P, 4 * 4 * 64], I32, name="w2_codes", align_bytes=64)
-        w2_planes = keep.tile([P, 4 * 4 * 32], I32, name="w2_planes", tag="early_table", align_bytes=64)
+        w2_planes = stage.tile([P, 4 * 4 * 32], I32, name="w2_planes", offset=16384, align_bytes=64)
         nc.vector.tensor_copy(
             w2_codes[:].rearrange("p (x t q w) -> p x t q w", x=4, t=4, w=4),
             w2_raw[:].rearrange("p a n -> p (a n)").rearrange("p (x q t w) -> p x t q w", x=4, t=4, w=4),
         )
         load_w1(1, 0)
 
-        first_words = keep.tile([P, S], U32, name="first_words", tag="window", align_bytes=64)
-        nc.vector.tensor_copy(first_words[:], table[0][:].bitcast(U32).indirect(offs_t[:]))
-        v_words = {(0, h): first_words[:, HALF * h : HALF * (h + 1)] for h in range(2)}
-        nc.vector.tensor_copy(
-            w2_planes[:].rearrange("p (x t q w) -> p x t q w", x=4, t=4, w=2),
-            w2_scale_raw[:].rearrange("p a n -> p (a n)").rearrange("p (x q t w) -> p x t q w", x=4, t=4, w=2),
-        )
+        v_words = {}
         for h in range(2):
-            picked = keep.tile([P, HALF], U32, name="second_words%d" % h, align_bytes=64)
-            nc.vector.tensor_copy(picked[:], table[1][:].bitcast(U32).indirect(offs_t[:, 32 * h : 32 * (h + 1)]))
-            v_words[1, h] = picked[:]
+            for a in range(2):
+                tag = "window" if (a, h) == (0, 0) else "v_words%d%d" % (a, h)
+                if (a, h) == (0, 1):
+                    tag = "late"
+                picked = keep.tile([P, HALF], U32, name="v_words", tag=tag, align_bytes=64)
+                nc.vector.tensor_copy(picked[:], table[a][:].bitcast(U32).indirect(offs_t[:, 32 * h : 32 * (h + 1)]))
+                v_words[a, h] = picked[:]
+                if (a, h) == (0, 0):
+                    nc.vector.tensor_copy(
+                        w2_planes[:].rearrange("p (x t q w) -> p x t q w", x=4, t=4, w=2),
+                        w2_scale_raw[:].rearrange("p a n -> p (a n)").rearrange("p (x q t w) -> p x t q w", x=4, t=4, w=2),
+                    )
 
         def product(u, h, tag, codes, planes):
             acc = psum.tile([P, HALF], F32, name="acc", tag=tag)
@@ -146,25 +152,24 @@ def tile_list_string_soiling_features_kernel(
                 sq = ring.tile([P, S], F32, name="sq")
             else:
                 sq = keep.tile([P, S], F32, name="sq_last", tag="last")
+            if u < 2:
+                rec_tile = keep.tile([P, 2, HALF], F32, name="damp%d" % u)
+                rec = rec_tile[:]
+            else:
+                rec = picks[(u - 1) // 4][:, (u - 1) % 4, :, :]
             for h in range(2):
                 acc = product(
                     u, h, "pb",
                     lambda a: w2c[:, 2 * first(a) : 2 * (first(a) + P)].bitcast(FP4X4),
                     lambda a: w2p[:, first(a) : first(a) + P],
                 )
-                nc.scalar.activation(out=sq[:, HALF * h : HALF * (h + 1)], in_=acc[:], func=ACT.Square)
-            width = HALF if u == 0 else S
-            for c in range(0, S, width):
-                cols = slice(c, c + width)
-                nc.scalar.activation(out=sq[:, cols], in_=sq[:, cols], func=ACT.Abs_reciprocal_sqrt, bias=1.0)
-            if u < 2:
-                rec = keep.tile([P, 2, HALF], F32, name="damp%d" % u)[:]
-            else:
-                rec = picks[(u - 1) // 4][:, (u - 1) % 4, :, :]
-            if u == 0:
-                for h in range(2):
-                    nc.scalar.activation(out=rec[:, h, :], in_=sq[:, HALF * h : HALF * (h + 1)], func=ACT.Square)
-            else:
+                cols = slice(HALF * h, HALF * (h + 1))
+                nc.scalar.activation(out=sq[:, cols], in_=acc[:], func=ACT.Square)
+                if u == 0:
+                    nc.scalar.activation(out=sq[:, cols], in_=sq[:, cols], func=ACT.Abs_reciprocal_sqrt, bias=1.0)
+                    nc.scalar.activation(out=rec[:, h, :], in_=sq[:, cols], func=ACT.Square)
+            if u > 0:
+                nc.scalar.activation(out=sq[:], in_=sq[:], func=ACT.Abs_reciprocal_sqrt, bias=1.0)
                 nc.scalar.activation(out=rec, in_=sq[:].rearrange("p (h c) -> p h c", h=2), func=ACT.Square)
             damp[u] = rec
 
@@ -175,7 +180,7 @@ def tile_list_string_soiling_features_kernel(
         def round_w1(u, a, copy):
             b, t = divmod(u, 4)
             if a == 0:
-                w1_grouped[u] = ring.tile([P, 2, HALF], BF16, name="w1_grouped", bufs=4, align_bytes=64)
+                w1_grouped[u] = ring.tile([P, 2, HALF], BF16, name="w1_grouped", bufs=8, align_bytes=64)
             if copy is None:
                 nc.gpsimd.tensor_scalar(
                     w1_grouped[u][:, a, :].rearrange("p (q i j) -> p q i j", i=8, j=4),
@@ -190,8 +195,8 @@ def tile_list_string_soiling_features_kernel(
 
         def quantize_w1(u):
             grouped = w1_grouped[u]
-            codes = keep.tile([P, 2 * P], U32, name="w1_codes%d" % u, align_bytes=64)
-            planes = keep.tile([P, 2 * P], U8, name="w1_planes%d" % u, align_bytes=64)
+            codes = keep.tile([P, 2 * P], U32, name="w1_codes", tag="codes%d" % min(u, 3), align_bytes=64)
+            planes = keep.tile([P, 2 * P], U8, name="w1_planes", tag="planes%d" % min(u, 3), align_bytes=64)
             nc.vector.quantize_mx(
                 out=codes[:].bitcast(FP8X4), scales=planes[:], in_=grouped[:].rearrange("p a c -> p (a c)")
             )
@@ -220,22 +225,30 @@ def tile_list_string_soiling_features_kernel(
 
         w3_q = {}
 
-        def quantize_w3(b):
+        w3_grouped = {}
+
+        def round_w3(b):
             raw = staging(b)
             rows = w3[HALF * b : HALF * (b + 1), :].rearrange("(q t i) n -> i q t n", t=4, i=8)
             for i in range(8):
                 nc.sync.dma_start(raw[i:P:8, :, :], rows[i])
             grouped = ring.tile([P, 4 * N], BF16, name="w3_grouped", align_bytes=64)
-            nc.scalar.copy(
-                grouped[:].rearrange("k (s p j) -> k p j s", s=4, j=4),
-                raw[:].rearrange("k j (p s) -> k p j s", s=4),
-            )
-            codes = keep.tile([P, N], U32, name="w3_codes%d" % b, align_bytes=64)
-            planes = keep.tile([P, N], U8, name="w3_planes%d" % b, align_bytes=64)
+            for s in range(4):
+                nc.gpsimd.tensor_scalar(
+                    grouped[:, N * s : N * (s + 1)].rearrange("k (p j) -> k p j", j=4),
+                    raw[:].rearrange("k j (p s) -> k s p j", s=4)[:, s],
+                    1.0, 0.0, MULT, ADD,
+                )
+            w3_grouped[b] = grouped
+
+        def quantize_w3(b):
+            grouped = w3_grouped[b]
+            codes = keep.tile([P, N], U32, name="w3_codes", tag=("codes3", "w3_codes")[b], align_bytes=64)
+            planes = keep.tile([P, N], U8, name="w3_planes", tag=("w3_planes", "planes3")[b], align_bytes=64)
             nc.vector.quantize_mx(out=codes[:].bitcast(FP8X4), scales=planes[:], in_=grouped[:])
             w3_q[b] = (codes, planes)
 
-        for u in range(4):
+        for u in range(2):
             round_w1(u, 0, nc.scalar.copy)
         damping(0)
         damping(1)
@@ -249,10 +262,17 @@ def tile_list_string_soiling_features_kernel(
             nc.sync.dma_start(gain_rows[4 * b : 4 * b + 4, :].rearrange("t (q i) -> t q i", i=8), gain_view[b])
 
         for u in range(4):
+            if u >= 2:
+                round_w1(u, 0, None)
             round_w1(u, 1, nc.vector.tensor_copy)
             quantize_w1(u)
         load_w1(0, 1)
         load_w1(1, 1)
+        for u in range(4, 8):
+            round_w1(u, 0, None)
+            round_w1(u, 1, None)
+        round_w3(0)
+        round_w3(1)
         for u in range(8):
             if u + 2 < 8:
                 damping(u + 2)
@@ -261,19 +281,20 @@ def tile_list_string_soiling_features_kernel(
                 pick(0)
             if u >= 2:
                 pick(u - 1)
-            if u < 4:
-                round_w1(4 + u, 0, None)
-                round_w1(4 + u, 1, None)
-                quantize_w1(4 + u)
+            if 3 <= u < 7:
+                quantize_w1(u + 1)
             if u == 5:
                 turned = psum.tile([P, P], F32, name="turned", tag="pb")
                 nc.tensor.transpose(turned[:], gain_rows[:], identity[:])
                 gains = keep.tile([P, 8], F32, name="gains", tag="last")
                 nc.scalar.copy(gains[:], turned[:, 0:8])
 
+        quantize_w3(0)
+        quantize_w3(1)
         pick(7)
 
-        z_q = []
+        width = M // 2
+        sums = {}
         for b in range(2):
             bounded = ring.tile([P, 4, M], F32, name="bounded")
             for t in range(4):
@@ -281,51 +302,50 @@ def tile_list_string_soiling_features_kernel(
                 nc.scalar.activation(
                     out=bounded[:, t, :], in_=picks[b][:, t, 0, :], func=ACT.Tanh, scale=gains[:, u : u + 1]
                 )
-            if b == 0:
-                quantize_w3(0)
-                quantize_w3(1)
-            codes = keep.tile([P, M], U32, name="z_codes%d" % b, align_bytes=64)
-            planes = keep.tile([P, M], U8, name="z_planes%d" % b, align_bytes=64)
-            width = M if b == 0 else CHUNK
-            for c in range(M // width):
+            for c in range(2):
                 cols = slice(width * c, width * (c + 1))
-                z = ring.tile([P, 4 * width], BF16, name="z", tag="z%d" % b, bufs=1 + 3 * b, align_bytes=64)
+                z = ring.tile([P, 4 * width], BF16, name="z", align_bytes=64)
                 nc.vector.tensor_tensor(
-                    z[:].rearrange("p (c i t) -> p c t i", i=4, t=4),
-                    bounded[:, :, cols].rearrange("p t (c i) -> p c t i", i=4),
-                    picks[b][:, :, 1, cols].rearrange("p t (c i) -> p c t i", i=4),
+                    z[:].rearrange("p (c i t) -> p c t i", i=2, t=4),
+                    bounded[:, :, cols].rearrange("p t (c i) -> p c t i", i=2),
+                    picks[b][:, :, 1, cols].rearrange("p t (c i) -> p c t i", i=2),
                     MULT,
                 )
-                nc.vector.quantize_mx(out=codes[:, cols].bitcast(FP8X4), scales=planes[:, cols], in_=z[:])
-            z_q.append((codes, planes))
+                codes = ring.tile([P, width], U32, name="z_codes", bufs=4, align_bytes=64)
+                planes = ring.tile([P, width], U8, name="z_planes", bufs=4, align_bytes=64)
+                nc.vector.quantize_mx(out=codes[:].bitcast(FP8X4), scales=planes[:], in_=z[:])
+                for s in range(4):
+                    if b == 0:
+                        sums[c, s] = psum.tile([P, width], F32, name="y_sum", tag=("pa", "pb")[c])
+                    nc.tensor.matmul_mx(
+                        out=sums[c, s][:],
+                        lhsT=w3_q[b][0][:, P * s : P * (s + 1)].bitcast(FP8X4),
+                        lhsT_scale=w3_q[b][1][:, P * s : P * (s + 1)],
+                        rhs=codes[:].bitcast(FP8X4),
+                        rhs_scale=planes[:],
+                        start=(b == 0),
+                        stop=(b == 1),
+                    )
 
         y_codes = keep.tile([P, M], U32, name="y_codes", align_bytes=64)
         y_planes = keep.tile([P, M], U8, name="y_planes", align_bytes=64)
         out_rows = out_0.rearrange("(p s) m -> p s m", s=4)
         out_words = out_1[0].rearrange("p m t -> p (m t)").bitcast(I32)
-        for c in range(M // CHUNK):
-            cols = slice(CHUNK * c, CHUNK * (c + 1))
-            acc = psum.tile([P, 4, CHUNK], F32, name="y_acc", tag="pb")
+        for c in range(2):
+            cols = slice(width * c, width * (c + 1))
+            y = ring.tile([P, 4, width], F32, name="y")
             for s in range(4):
-                for b in range(2):
-                    nc.tensor.matmul_mx(
-                        out=acc[:, s, :],
-                        lhsT=w3_q[b][0][:, P * s : P * (s + 1)].bitcast(FP8X4),
-                        lhsT_scale=w3_q[b][1][:, P * s : P * (s + 1)],
-                        rhs=z_q[b][0][:, cols].bitcast(FP8X4),
-                        rhs_scale=z_q[b][1][:, cols],
-                        start=(b == 0),
-                        stop=(b == 1),
-                    )
-            y = ring.tile([P, 4, CHUNK], F32, name="y", bufs=4)
-            nc.scalar.copy(y[:], acc[:])
+                copy = nc.vector.tensor_copy if (c == 1 and s >= 2) else nc.scalar.copy
+                copy(y[:, s, :], sums[c, s][:])
             nc.sync.dma_start(out_rows[:, :, cols], y[:])
-            y_grouped = ring.tile([P, 4 * CHUNK], BF16, name="y_grouped", bufs=4, align_bytes=64)
-            nc.vector.tensor_copy(
-                y_grouped[:].rearrange("p (c i s) -> p c s i", i=4, s=4),
-                y[:].rearrange("p s (c i) -> p c s i", i=4),
-            )
-            nc.vector.quantize_mx(out=y_codes[:, cols].bitcast(FP8X4), scales=y_planes[:, cols], in_=y_grouped[:])
+            for x in range(2):
+                part = slice(width * c + CHUNK * x, width * c + CHUNK * (x + 1))
+                y_grouped = ring.tile([P, 4 * CHUNK], BF16, name="y_grouped", bufs=4, align_bytes=64)
+                nc.vector.tensor_copy(
+                    y_grouped[:].rearrange("p (c i s) -> p c s i", i=4, s=4),
+                    y[:, :, CHUNK * x : CHUNK * (x + 1)].rearrange("p s (c i) -> p c s i", i=4),
+                )
+                nc.vector.quantize_mx(out=y_codes[:, part].bitcast(FP8X4), scales=y_planes[:, part], in_=y_grouped[:])
             nc.sync.dma_start(out_words[:, cols], y_codes[:, cols].bitcast(I32))
         for d in range(4):
             queue = nc.sync if d % 2 == 0 else nc.scalar

from contextlib import ExitStack

import concourse.mybir as mybir
from concourse.masks import make_identity

T, S, M, K, H, N = 2048, 1024, 512, 1024, 1024, 512
FLOPS = 2 * (2 * K * H * S + H * N * M)

F32 = mybir.dt.float32
BF16 = mybir.dt.bfloat16
I32 = mybir.dt.int32
U32 = mybir.dt.uint32
U16 = mybir.dt.uint16
U8 = mybir.dt.uint8
FP8X4 = mybir.dt.float8_e4m3fn_x4
FP4X4 = mybir.dt.float4_e2m1fn_x4
ACT = mybir.ActivationFunctionType
MULT = mybir.AluOpType.mult
ADD = mybir.AluOpType.add

P = 128
HALF = 512
CHUNK = 128


def tile_list_string_soiling_features_kernel(
    tc, tab_words, tab_scales, offs, pos1, pos2, w1, w2_words, w2_scales, gain, w3, out_0, out_1, out_2
):
    nc = tc.nc
    with ExitStack() as ctx:
        lists = ctx.enter_context(tc.tile_pool(name="lists", bufs=1))
        keep = ctx.enter_context(tc.tile_pool(name="keep", bufs=1))
        ring = ctx.enter_context(tc.tile_pool(name="ring", bufs=2))
        stage = ctx.enter_context(tc.tile_pool(name="stage", bufs=1))
        psum = ctx.enter_context(tc.psum_pool(name="psum", bufs=4))

        offs_t = lists.tile([P, S // 16], U16, name="offs_t")
        pos1_t = lists.tile([P, M // 16], U16, name="pos1_t")
        pos2_t = lists.tile([P, M // 16], U16, name="pos2_t")
        scale_window = keep.tile([P, T], U8, name="scale_window", tag="window", align_bytes=64)
        w2_scale_raw = keep.tile([P, 2, H // 4], I32, name="w2_scale_raw", tag="late", align_bytes=64)
        v_scales = [keep.tile([P, S], U8, name="v_scales%d" % a, align_bytes=64) for a in range(2)]
        warm_in = keep.tile([P, 1], F32, name="warm_in", tag="late_table")
        warm_bias = stage.tile([P, 1], F32, name="warm_bias", offset=0)
        warm_out = stage.tile([P, 1], F32, name="warm_out", offset=14336)

        nc.gpsimd.memset(scale_window[:].bitcast(I32), 0)
        nc.vector.memset(warm_in[:], 1.0)
        nc.vector.memset(warm_bias[:], 1.0)
        nc.vector.memset(w2_scale_raw[:], 0)
        nc.vector.memset(v_scales[1][:].bitcast(I32), 0)

        nc.sync.dma_start(offs_t[:], offs)
        nc.sync.dma_start(pos1_t[:], pos1)
        nc.sync.dma_start(pos2_t[:], pos2)
        for a in range(2):
            rows = tab_scales[a].bitcast(I32).rearrange("(g e) n -> e g n", e=2)
            for e in range(2):
                nc.scalar.dma_start(scale_window[:].bitcast(I32)[2 * a + e : P : 16, :], rows[e])
        nc.scalar.activation(out=warm_out[:], in_=warm_in[:], func=ACT.Abs_reciprocal_sqrt, bias=warm_bias[:])

        w1_raw = {}

        def staging(x):
            return stage.tile([P, 4, HALF], F32, name="raw", tag="raw%d" % x, offset=8192 * x)

        def load_w1(a, b):
            if b == 0:
                raw = staging(a)
            else:
                raw = keep.tile([P, 4, HALF], F32, name="w1_late", tag=("early_table", "late_table")[a])
            rows = w1[HALF * a : HALF * (a + 1), HALF * b : HALF * (b + 1)]
            nc.sync.dma_start(raw[:], rows.rearrange("(p j) c -> p j c", j=4))
            w1_raw[a, b] = raw

        table = [
            keep.tile([P, T], I32, name="table0", tag="early_table"),
            keep.tile([P, T], I32, name="table1", tag="late_table"),
        ]
        w2_raw = stage.tile([P, 2, H // 2], I32, name="w2_raw", offset=14336)
        nc.sync.dma_start(table[0][:], tab_words[0].rearrange("p t i -> p (t i)").bitcast(I32))
        nc.sync.dma_start(w2_raw[:], w2_words.bitcast(I32).rearrange("a p n -> p a n"))
        nc.sync.dma_start(table[1][:], tab_words[1].rearrange("p t i -> p (t i)").bitcast(I32))
        load_w1(0, 0)
        for d in range(4):
            nc.gpsimd.dma_start(
                w2_scale_raw[32 * d : 32 * d + 4, :, :],
                w2_scales.bitcast(I32)[:, 4 * d : 4 * d + 4, :].rearrange("a r n -> r a n"),
            )

        picked_scales = keep.tile([P, S], U8, name="picked_scales", tag="picked", align_bytes=64)
        nc.vector.tensor_copy(picked_scales[:], scale_window[:].indirect(offs_t[:]))
        picked32 = picked_scales[:].bitcast(I32)
        nc.vector.tensor_copy(v_scales[0][:].bitcast(I32), picked32)

        for a in (1, 0):
            for h in range(2):
                if a == 0 and h == 0:
                    continue
                for e in range(2):
                    nc.scalar.dma_start(
                        v_scales[a][:].bitcast(I32)[2 * h + e : P : 32, :],
                        picked32[16 * h + 2 * a + e : P : 32, :],
                    )

        w2_codes = keep.tile([P, 4 * 4 * 64], I32, name="w2_codes", align_bytes=64)
        w2_planes = stage.tile([P, 4 * 4 * 32], I32, name="w2_planes", offset=16384, align_bytes=64)
        nc.vector.tensor_copy(
            w2_codes[:].rearrange("p (x t q w) -> p x t q w", x=4, t=4, w=4),
            w2_raw[:].rearrange("p a n -> p (a n)").rearrange("p (x q t w) -> p x t q w", x=4, t=4, w=4),
        )
        load_w1(1, 0)

        v_words = {}
        for h in range(2):
            for a in range(2):
                tag = "window" if (a, h) == (0, 0) else "v_words%d%d" % (a, h)
                if (a, h) == (0, 1):
                    tag = "late"
                picked = keep.tile([P, HALF], U32, name="v_words", tag=tag, align_bytes=64)
                nc.vector.tensor_copy(picked[:], table[a][:].bitcast(U32).indirect(offs_t[:, 32 * h : 32 * (h + 1)]))
                v_words[a, h] = picked[:]
                if (a, h) == (0, 0):
                    nc.vector.tensor_copy(
                        w2_planes[:].rearrange("p (x t q w) -> p x t q w", x=4, t=4, w=2),
                        w2_scale_raw[:].rearrange("p a n -> p (a n)").rearrange("p (x q t w) -> p x t q w", x=4, t=4, w=2),
                    )

        def product(u, h, tag, codes, planes):
            acc = psum.tile([P, HALF], F32, name="acc", tag=tag)
            for a in range(2):
                nc.tensor.matmul_mx(
                    out=acc[:],
                    lhsT=codes(a),
                    lhsT_scale=planes(a),
                    rhs=v_words[a, h].bitcast(FP8X4),
                    rhs_scale=v_scales[a][:, HALF * h : HALF * (h + 1)],
                    start=(a == 0),
                    stop=(a == 1),
                )
            return acc

        damp = {}
        picks = [keep.tile([P, 4, 2, M], F32, name="picks%d" % b) for b in range(2)]

        def damping(u):
            b, t = divmod(u, 4)
            w2c = w2_codes[:].bitcast(U8)
            w2p = w2_planes[:].bitcast(U8)
            first = lambda a: (8 * a + u) * P
            if u < 7:
                sq = ring.tile([P, S], F32, name="sq")
            else:
                sq = keep.tile([P, S], F32, name="sq_last", tag="last")
            if u < 2:
                rec_tile = keep.tile([P, 2, HALF], F32, name="damp%d" % u)
                rec = rec_tile[:]
            else:
                rec = picks[(u - 1) // 4][:, (u - 1) % 4, :, :]
            for h in range(2):
                acc = product(
                    u, h, "pb",
                    lambda a: w2c[:, 2 * first(a) : 2 * (first(a) + P)].bitcast(FP4X4),
                    lambda a: w2p[:, first(a) : first(a) + P],
                )
                cols = slice(HALF * h, HALF * (h + 1))
                nc.scalar.activation(out=sq[:, cols], in_=acc[:], func=ACT.Square)
                if u == 0:
                    nc.scalar.activation(out=sq[:, cols], in_=sq[:, cols], func=ACT.Abs_reciprocal_sqrt, bias=1.0)
                    nc.scalar.activation(out=rec[:, h, :], in_=sq[:, cols], func=ACT.Square)
            if u > 0:
                nc.scalar.activation(out=sq[:], in_=sq[:], func=ACT.Abs_reciprocal_sqrt, bias=1.0)
                nc.scalar.activation(out=rec, in_=sq[:].rearrange("p (h c) -> p h c", h=2), func=ACT.Square)
            damp[u] = rec

        w1_q = {}

        w1_grouped = {}

        def round_w1(u, a, copy):
            b, t = divmod(u, 4)
            if a == 0:
                w1_grouped[u] = ring.tile([P, 2, HALF], BF16, name="w1_grouped", bufs=8, align_bytes=64)
            if copy is None:
                nc.gpsimd.tensor_scalar(
                    w1_grouped[u][:, a, :].rearrange("p (q i j) -> p q i j", i=8, j=4),
                    w1_raw[a, b][:].rearrange("p j (q t i) -> p t q i j", t=4, i=8)[:, t],
                    1.0, 0.0, MULT, ADD,
                )
                return
            copy(
                w1_grouped[u][:, a, :].rearrange("p (q x i j) -> p q x j i", x=2, i=4, j=4),
                w1_raw[a, b][:].rearrange("p j (q t x i) -> p t q x j i", t=4, x=2, i=4)[:, t],
            )

        def quantize_w1(u):
            grouped = w1_grouped[u]
            codes = keep.tile([P, 2 * P], U32, name="w1_codes", tag="codes%d" % min(u, 3), align_bytes=64)
            planes = keep.tile([P, 2 * P], U8, name="w1_planes", tag="planes%d" % min(u, 3), align_bytes=64)
            nc.vector.quantize_mx(
                out=codes[:].bitcast(FP8X4), scales=planes[:], in_=grouped[:].rearrange("p a c -> p (a c)")
            )
            w1_q[u] = (codes, planes)


        h_tiles = {}

        def channels(u):
            b, t = divmod(u, 4)
            codes, planes = w1_q[u]
            h_all = ring.tile([P, S], F32, name="h_all", bufs=3)
            for h in range(2):
                acc = product(
                    u, h, "pa",
                    lambda a: codes[:, P * a : P * (a + 1)].bitcast(FP8X4),
                    lambda a: planes[:, P * a : P * (a + 1)],
                )
                nc.vector.tensor_tensor(h_all[:, HALF * h : HALF * (h + 1)], acc[:], damp[u][:, h, :], MULT)
            h_tiles[u] = h_all

        def pick(u):
            b, t = divmod(u, 4)
            nc.vector.tensor_copy(picks[b][:, t, 0, :], h_tiles[u][:].indirect(pos1_t[:]))
            nc.vector.tensor_copy(picks[b][:, t, 1, :], h_tiles[u][:].indirect(pos2_t[:]))

        w3_q = {}

        w3_grouped = {}

        def round_w3(b):
            raw = staging(b)
            rows = w3[HALF * b : HALF * (b + 1), :].rearrange("(q t i) n -> i q t n", t=4, i=8)
            for i in range(8):
                nc.sync.dma_start(raw[i:P:8, :, :], rows[i])
            grouped = ring.tile([P, 4 * N], BF16, name="w3_grouped", align_bytes=64)
            for s in range(4):
                nc.gpsimd.tensor_scalar(
                    grouped[:, N * s : N * (s + 1)].rearrange("k (p j) -> k p j", j=4),
                    raw[:].rearrange("k j (p s) -> k s p j", s=4)[:, s],
                    1.0, 0.0, MULT, ADD,
                )
            w3_grouped[b] = grouped

        def quantize_w3(b):
            grouped = w3_grouped[b]
            codes = keep.tile([P, N], U32, name="w3_codes", tag=("codes3", "w3_codes")[b], align_bytes=64)
            planes = keep.tile([P, N], U8, name="w3_planes", tag=("w3_planes", "planes3")[b], align_bytes=64)
            nc.vector.quantize_mx(out=codes[:].bitcast(FP8X4), scales=planes[:], in_=grouped[:])
            w3_q[b] = (codes, planes)

        for u in range(2):
            round_w1(u, 0, nc.scalar.copy)
        damping(0)
        damping(1)

        identity = keep.tile([P, P], F32, name="identity")
        make_identity(nc, identity[:])
        gain_rows = keep.tile([P, P], F32, name="gain_rows", tag="picked", align_bytes=64)
        nc.gpsimd.memset(gain_rows[:], 0.0)
        gain_view = gain.rearrange("(b q t i) -> b t q i", b=2, t=4, i=8)
        for b in range(2):
            nc.sync.dma_start(gain_rows[4 * b : 4 * b + 4, :].rearrange("t (q i) -> t q i", i=8), gain_view[b])

        for u in range(4):
            if u >= 2:
                round_w1(u, 0, None)
            round_w1(u, 1, nc.vector.tensor_copy)
            quantize_w1(u)
        load_w1(0, 1)
        load_w1(1, 1)
        for u in range(4, 8):
            round_w1(u, 0, None)
            round_w1(u, 1, None)
        round_w3(0)
        round_w3(1)
        for u in range(8):
            if u + 2 < 8:
                damping(u + 2)
            channels(u)
            if u == 0:
                pick(0)
            if u >= 2:
                pick(u - 1)
            if 3 <= u < 7:
                quantize_w1(u + 1)
            if u == 5:
                turned = psum.tile([P, P], F32, name="turned", tag="pb")
                nc.tensor.transpose(turned[:], gain_rows[:], identity[:])
                gains = keep.tile([P, 8], F32, name="gains", tag="last")
                nc.scalar.copy(gains[:], turned[:, 0:8])

        quantize_w3(0)
        quantize_w3(1)
        pick(7)

        width = M // 2
        sums = {}
        for b in range(2):
            bounded = ring.tile([P, 4, M], F32, name="bounded")
            for t in range(4):
                u = 4 * b + t
                nc.scalar.activation(
                    out=bounded[:, t, :], in_=picks[b][:, t, 0, :], func=ACT.Tanh, scale=gains[:, u : u + 1]
                )
            for c in range(2):
                cols = slice(width * c, width * (c + 1))
                z = ring.tile([P, 4 * width], BF16, name="z", align_bytes=64)
                nc.vector.tensor_tensor(
                    z[:].rearrange("p (c i t) -> p c t i", i=2, t=4),
                    bounded[:, :, cols].rearrange("p t (c i) -> p c t i", i=2),
                    picks[b][:, :, 1, cols].rearrange("p t (c i) -> p c t i", i=2),
                    MULT,
                )
                codes = ring.tile([P, width], U32, name="z_codes", bufs=4, align_bytes=64)
                planes = ring.tile([P, width], U8, name="z_planes", bufs=4, align_bytes=64)
                nc.vector.quantize_mx(out=codes[:].bitcast(FP8X4), scales=planes[:], in_=z[:])
                for s in range(4):
                    if b == 0:
                        sums[c, s] = psum.tile([P, width], F32, name="y_sum", tag=("pa", "pb")[c])
                    nc.tensor.matmul_mx(
                        out=sums[c, s][:],
                        lhsT=w3_q[b][0][:, P * s : P * (s + 1)].bitcast(FP8X4),
                        lhsT_scale=w3_q[b][1][:, P * s : P * (s + 1)],
                        rhs=codes[:].bitcast(FP8X4),
                        rhs_scale=planes[:],
                        start=(b == 0),
                        stop=(b == 1),
                    )

        y_codes = keep.tile([P, M], U32, name="y_codes", align_bytes=64)
        y_planes = keep.tile([P, M], U8, name="y_planes", align_bytes=64)
        out_rows = out_0.rearrange("(p s) m -> p s m", s=4)
        out_words = out_1[0].rearrange("p m t -> p (m t)").bitcast(I32)
        for c in range(2):
            cols = slice(width * c, width * (c + 1))
            y = ring.tile([P, 4, width], F32, name="y")
            for s in range(4):
                copy = nc.vector.tensor_copy if (c == 1 and s >= 2) else nc.scalar.copy
                copy(y[:, s, :], sums[c, s][:])
            nc.sync.dma_start(out_rows[:, :, cols], y[:])
            for x in range(2):
                part = slice(width * c + CHUNK * x, width * c + CHUNK * (x + 1))
                y_grouped = ring.tile([P, 4 * CHUNK], BF16, name="y_grouped", bufs=4, align_bytes=64)
                nc.vector.tensor_copy(
                    y_grouped[:].rearrange("p (c i s) -> p c s i", i=4, s=4),
                    y[:, :, CHUNK * x : CHUNK * (x + 1)].rearrange("p s (c i) -> p c s i", i=4),
                )
                nc.vector.quantize_mx(out=y_codes[:, part].bitcast(FP8X4), scales=y_planes[:, part], in_=y_grouped[:])
            nc.sync.dma_start(out_words[:, cols], y_codes[:, cols].bitcast(I32))
        for d in range(4):
            queue = nc.sync if d % 2 == 0 else nc.scalar
            queue.dma_start(
                out_2[0].bitcast(I32)[4 * d : 4 * d + 4, :], y_planes[:].bitcast(I32)[32 * d : 32 * d + 4, :]
            )
